import numpy as np
import ml_dtypes


def mxq(x, axis, fmt="e4m3"):
    dtype, down = {"e4m3": (ml_dtypes.float8_e4m3fn, 7), "e5m2": (ml_dtypes.float8_e5m2, 14)}[fmt]
    v = np.moveaxis(np.asarray(x, np.float32).astype(ml_dtypes.bfloat16).astype(np.float64), axis, -1)
    blocks = v.reshape(v.shape[:-1] + (-1, 32))
    amax = np.abs(blocks).max(-1, keepdims=True)
    byte = np.maximum(np.where(amax > 0, np.frexp(amax)[1] - 1 + 127, 0) - down, 1)
    scale = np.exp2(byte - 127.0)
    codes = (blocks / scale).astype(np.float32).astype(dtype).astype(np.float64)
    return np.moveaxis((codes * scale).reshape(v.shape), -1, axis)


WIDE = False


def mx_kscale(k):
    if not WIDE:
        return np.ones(k)
    levels = np.array([10, -10, 5, -5, 0])
    if k % 512:
        return np.exp2(np.random.permutation(np.resize(levels, k // 32))).repeat(32)
    a = np.empty((k // 512, 16))
    for p in range(k // 512):
        a[p, :8] = np.random.permutation(np.resize(levels, 8))
        for g in range(8):
            far = levels[np.abs(levels - a[p, g]) >= 10]
            a[p, g + 8] = far[np.random.randint(len(far))]
    return np.exp2(a.ravel()).repeat(32)


def f64(x):
    return np.asarray(x).astype(np.float64)


def striped(idx):
    return np.tile(idx.reshape(-1, 16).T, (8, 1)).astype(np.uint16)


def unstriped(offs):
    return offs[:16].T.reshape(-1).astype(np.int64)


def striped8(idx):
    return np.concatenate([x.reshape(-1, 16).T for x in idx]).astype(np.uint16)


def runs(offs, k):
    lists = np.stack([offs[16 * r : 16 * r + 16].T.reshape(-1) for r in range(8)]).astype(np.int64)
    return lists[np.arange(k) % 512 // 64]


def pack_weight(w):
    k, n = w.shape
    w = f64(np.asarray(w, np.float32).astype(ml_dtypes.bfloat16)).reshape(k // 32, 32, n)
    amax = np.abs(w).max(1)
    byte = np.clip(np.where(amax > 0, np.frexp(amax)[1] - 1 + 127 - 7, 1), 1, 254)
    scaled = (w * np.exp2(127.0 - byte)[:, None, :]).reshape(k, n).astype(np.float32)
    words = np.ascontiguousarray(scaled.reshape(k // 512, 128, 4, n).transpose(0, 1, 3, 2)).astype(ml_dtypes.float8_e4m3fn).view(np.uint8)
    return words, np.ascontiguousarray(byte.astype(np.uint8).reshape(k // 512, 16, n))


def unpack_weight(words, scales):
    g, p, n, _ = words.shape
    vals = np.ascontiguousarray(words).view(ml_dtypes.float8_e4m3fn).astype(np.float64) * np.repeat(np.exp2(scales.astype(np.float64) - 127.0), 8, axis=1)[..., None]
    return vals.transpose(0, 1, 3, 2).reshape(g * 512, n)


E2M1 = np.array([0.0, 0.5, 1.0, 1.5, 2.0, 3.0, 4.0, 6.0, -0.0, -0.5, -1.0, -1.5, -2.0, -3.0, -4.0, -6.0])


def pack_fp4(w):
    k, n = w.shape
    w = f64(np.asarray(w, np.float32).astype(ml_dtypes.bfloat16)).reshape(k // 32, 32, n)
    amax = np.abs(w).max(1)
    mant, ex = np.frexp(amax / 6.0)
    byte = np.clip(np.where(amax > 0, np.where(mant > 0.5, ex, ex - 1) + 127, 1), 1, 254)
    scaled = (w * np.exp2(127.0 - byte)[:, None, :]).reshape(k, n).astype(np.float32)
    c = np.ascontiguousarray(scaled.reshape(k // 512, 128, 4, n).transpose(0, 1, 3, 2)).astype(ml_dtypes.float4_e2m1fn).view(np.uint8) & 0xF
    words = (c[..., 0::2] | (c[..., 1::2] << 4)).reshape(k // 512, 128, 2 * n)
    return np.ascontiguousarray(words), np.ascontiguousarray(byte.astype(np.uint8).reshape(k // 512, 16, n))


def unpack_fp4(words, scales):
    g, _, n = scales.shape
    words = np.ascontiguousarray(words).reshape(g, 128, n, 2)
    nib = np.empty((g, 128, n, 4), np.uint8)
    nib[..., 0::2] = words & 0xF
    nib[..., 1::2] = words >> 4
    vals = E2M1[nib] * np.repeat(np.exp2(scales.astype(np.float64) - 127.0), 8, axis=1)[..., None]
    return vals.transpose(0, 1, 3, 2).reshape(g * 512, n)


def planes(y):
    n, m = y.shape
    v = y.astype(np.float32).astype(ml_dtypes.bfloat16).astype(np.float64).reshape(n // 32, 32, m)
    top = np.abs(v).max(1)
    byte = np.clip(np.where(top > 0, np.frexp(top)[1] - 1 + 127 - 7, 1), 1, 254)
    codes = (v * np.exp2(127.0 - byte)[:, None, :]).reshape(n, m).astype(np.float32).astype(ml_dtypes.float8_e4m3fn).view(np.uint8)
    words = codes.reshape(n // 512, 128, 4, m).transpose(0, 1, 3, 2)
    return np.ascontiguousarray(words), np.ascontiguousarray(byte.astype(np.uint8).reshape(n // 512, 16, m))


K, T, S, V, H, U = 512, 2048, 512, 512, 512, 1024


def setup_inputs():
    n = np.random.standard_normal
    s = mx_kscale(K)[:, None]
    u = mx_kscale(S)
    packed_xT = pack_weight(n((K, T)) * s)
    packed_w1 = pack_fp4(n((K, H)) / np.sqrt(K) / s)
    packed_w2 = pack_fp4(n((K, H)) / np.sqrt(K) / s)
    return {
        "x_words": packed_xT[0],
        "x_scales": packed_xT[1],
        "w1_words": packed_w1[0],
        "w1_scales": packed_w1[1],
        "w2_words": packed_w2[0],
        "w2_scales": packed_w2[1],
        "ga": (np.random.uniform(0.5, 1.5, (H, 1)) * u[:, None]).astype(np.float32),
        "gb": (np.random.uniform(0.5, 1.5, (H, 1)) / u[:, None]).astype(np.float32),
        "old": n((S, U)).astype(np.float32),
        "offs": striped(np.random.permutation(T)[:S]),
        "two": striped(np.random.permutation(T)[:V]),
        "n1": striped8(np.stack([np.random.permutation(S) for _ in range(8)])),
        "nq": striped8(np.stack([np.random.permutation(V) for _ in range(8)])),
        "slot": striped8(np.stack([np.random.permutation(U)[:V] for _ in range(8)])),
    }


def reference(x_words, x_scales, w1_words, w1_scales, w2_words, w2_scales, ga, gb, old, offs, two, n1, nq, slot):
    xq = unpack_weight(x_words, x_scales)[:, unstriped(offs)]
    a = unpack_fp4(w1_words, w1_scales).T @ xq
    z = f64(ga) * (a[np.arange(H)[:, None], runs(n1, H)])
    x_two = unpack_weight(x_words, x_scales)[:, unstriped(two)]
    b = unpack_fp4(w2_words, w2_scales).T @ x_two
    z2 = f64(gb) * (b - (b[np.arange(H)[:, None], runs(nq, H)]))
    s = 0.0625 * ((mxq(z, 0, "e4m3").T @ mxq(z2, 0, "e4m3")))
    nw = 0.5 * (s + f64(old)[np.arange(S)[:, None], runs(slot, S)])
    out = f64(old).copy()
    out[np.arange(S)[:, None], runs(slot, S)] = nw
    return (out,) + planes(out)

@@ -1,0 +1,227 @@
+from contextlib import ExitStack
+
+import concourse.mybir as mybir
+from concourse.masks import make_identity
+
+F32 = mybir.dt.float32
+BF16 = mybir.dt.bfloat16
+I32 = mybir.dt.int32
+U32 = mybir.dt.uint32
+U16 = mybir.dt.uint16
+U8 = mybir.dt.uint8
+FP8X4 = mybir.dt.float8_e4m3fn_x4
+FP4X4 = mybir.dt.float4_e2m1fn_x4
+COPY = mybir.ActivationFunctionType.Copy
+MULT = mybir.AluOpType.mult
+ADD = mybir.AluOpType.add
+SUB = mybir.AluOpType.subtract
+
+P = 128
+T = 2048
+N = 512
+U = 1024
+HALF = N // 2
+FLOPS = 3 * 2 * 512 * 512 * 512
+
+
+def tile_picked_keyput_none_po_kernel(
+    tc, x_words, x_scales, w1_words, w1_scales, w2_words, w2_scales, ga, gb, old, offs, two, n1, nq, slot, out_0, out_1, out_2
+):
+    nc = tc.nc
+    with ExitStack() as ctx:
+        lists = ctx.enter_context(tc.tile_pool(name="lists", bufs=1))
+        sb = ctx.enter_context(tc.tile_pool(name="sb", bufs=1))
+        ps = ctx.enter_context(tc.psum_pool(name="ps", bufs=1))
+
+        def load_list(name, src):
+            tile = lists.tile([P, N // 16], U16, name=name)
+            nc.sync.dma_start(tile[:], src)
+            return tile
+
+        def load_scale_rows(eng, tile, src):
+            for q in range(4):
+                eng.dma_start(tile[32 * q : 32 * q + 4, :].bitcast(I32), src[0, 4 * q : 4 * q + 4, :].bitcast(I32))
+
+        xs = sb.tile([P, T], U8, name="xs", tag="xs", align_bytes=64)
+        nc.gpsimd.memset(xs[:].bitcast(I32), 0)
+        ws_raw = [sb.tile([P, N], U8, name="ws_raw%d" % i, tag="ws_raw%d" % i, align_bytes=64) for i in range(2)]
+        gains_rows = sb.tile([P, P], F32, name="gains_rows", tag="gains_rows", align_bytes=64)
+        nc.gpsimd.memset(gains_rows[:], 0.0)
+        nc.gpsimd.memset(ws_raw[0][:].bitcast(I32), 0)
+        nc.gpsimd.memset(ws_raw[1][:].bitcast(I32), 0)
+        ident = sb.tile([P, P], F32, name="ident", tag="ident", align_bytes=64)
+        make_identity(nc, ident[:])
+
+        offs_t = load_list("offs_t", offs)
+        two_t = load_list("two_t", two)
+        n1_t = load_list("n1_t", n1)
+        nq_t = load_list("nq_t", nq)
+        slot_t = load_list("slot_t", slot)
+        ww_raw = sb.tile([P, 2 * N], U8, name="ww_raw0", tag="ww_raw", align_bytes=64)
+        nc.sync.dma_start(ww_raw[:].bitcast(I32), w1_words[0].bitcast(I32))
+        xw = sb.tile([P, T], I32, name="xw", tag="xw", align_bytes=64)
+        nc.sync.dma_start(xw[:], x_words[0].rearrange("p c r -> p (c r)").bitcast(I32))
+        load_scale_rows(nc.scalar, xs, x_scales)
+        for i, g in enumerate((ga, gb)):
+            nc.scalar.dma_start(
+                gains_rows[4 * i : 4 * i + 4, :].rearrange("t (g q) -> t g q", q=8),
+                g.rearrange("(g t q) o -> t g (q o)", t=4, q=8),
+            )
+        load_scale_rows(nc.scalar, ws_raw[0], w1_scales)
+        load_scale_rows(nc.sync, ws_raw[1], w2_scales)
+        old_rows = old.rearrange("(p t) u -> t p u", t=4)
+        out_rows = out_0.rearrange("(p t) u -> t p u", t=4)
+        order = (2, 0, 1, 3)
+
+        gains_ps = ps.tile([P, N], F32, name="gains_ps", tag="bank0")
+        nc.tensor.transpose(gains_ps[:, 0:P], gains_rows[:], ident[:])
+        gains = sb.tile([P, 8], F32, name="gains", tag="gains", align_bytes=64)
+        nc.scalar.copy(gains[:], gains_ps[:, 0:8])
+
+        picked_w = [sb.tile([P, N], U32, name="picked_w0", tag="picked_w0", align_bytes=64)]
+        picked_s = [sb.tile([P, N], U8, name="picked_s%d" % i, tag="picked_s%d" % i, align_bytes=64) for i in range(2)]
+        ww = [sb.tile([P, 2 * N], U8, name="ww%d" % i, tag="ww%d" % i, align_bytes=64) for i in range(2)]
+        ws = [sb.tile([P, N], U8, name="ws%d" % i, tag="ws%d" % i, align_bytes=64) for i in range(2)]
+
+        def deal(dst, src, run):
+            nc.vector.tensor_copy(
+                dst[:].bitcast(I32).rearrange("p (t g q) -> p t g q", t=4, q=run),
+                src[:].bitcast(I32).rearrange("p (g t q) -> p t g q", t=4, q=run),
+            )
+
+        def project(i, bank0):
+            banks = []
+            for t in range(4):
+                bank = ps.tile([P, N], F32, name="proj%d_%d" % (i, t), tag="bank%d" % (bank0 + t))
+                nc.tensor.matmul_mx(
+                    out=bank[:],
+                    lhsT=ww[i][:, 2 * P * t : 2 * P * (t + 1)].bitcast(FP4X4),
+                    lhsT_scale=ws[i][:, P * t : P * (t + 1)],
+                    rhs=picked_w[i][:].bitcast(FP8X4),
+                    rhs_scale=picked_s[i][:],
+                    start=True,
+                    stop=True,
+                )
+                banks.append(bank)
+            return banks
+
+        for i, lst in enumerate((offs_t, two_t)):
+            nc.vector.tensor_copy(picked_s[i][:], xs[:].indirect(lst[:]))
+        nc.vector.tensor_copy(picked_w[0][:], xw[:].bitcast(U32).indirect(offs_t[:]))
+        deal(ww[0], ww_raw, 4)
+        ww_raw = sb.tile([P, 2 * N], U8, name="ww_raw1", tag="ww_raw", align_bytes=64)
+        nc.sync.dma_start(ww_raw[:].bitcast(I32), w2_words[0].bitcast(I32))
+        deal(ws[0], ws_raw[0], 2)
+        a_banks = project(0, 0)
+        picked_w.append(sb.tile([P, N], U32, name="picked_w1", tag="ws_raw0", align_bytes=64))
+        nc.vector.tensor_copy(picked_w[1][:], xw[:].bitcast(U32).indirect(two_t[:]))
+        deal(ww[1], ww_raw, 4)
+        deal(ws[1], ws_raw[1], 2)
+        b_banks = project(1, 4)
+
+        page = {}
+        for r, tag in zip(order, ("xs", "gains_rows", "xw", "ww_raw")):
+            page[r] = sb.tile([P, U], F32, name="page%d" % r, tag=tag, align_bytes=64)
+            nc.sync.dma_start(page[r][:], old_rows[r])
+
+        a_rows = [sb.tile([P, N], F32, name="a_rows%d" % t, tag="a_rows%d" % t, align_bytes=64) for t in range(4)]
+        b_rows = [sb.tile([P, N], F32, name="b_rows%d" % t, tag="b_rows%d" % t, align_bytes=64) for t in range(4)]
+        b_twin = [sb.tile([P, N], F32, name="b_twin%d" % t, tag="b_twin%d" % t, align_bytes=64) for t in range(4)]
+        for t in range(4):
+            nc.scalar.activation(a_rows[t][:], a_banks[t][:], COPY, scale=gains[:, t : t + 1])
+        for t in range(4):
+            nc.scalar.activation(b_rows[t][:], b_banks[t][:], COPY, scale=gains[:, 4 + t : 5 + t])
+            nc.scalar.activation(b_twin[t][:], b_banks[t][:], COPY, scale=gains[:, 4 + t : 5 + t])
+
+        half_old = {}
+
+        def fetch_old(t, tag):
+            half_old[t] = sb.tile([P, N], F32, name="half_old%d" % t, tag=tag, align_bytes=64)
+            nc.vector.tensor_scalar(half_old[t][:], page[t][:].indirect(slot_t[:]), 0.5, 0.0, MULT, ADD)
+
+        fetch_old(order[0], "half_old")
+
+        z_bf = sb.tile([P, 4, P, 4], BF16, name="z_bf", tag="z_bf", align_bytes=64)
+        z2_bf = sb.tile([P, N, 4], BF16, name="z2_bf", tag="z2_bf", align_bytes=64)
+        cols = HALF // 16
+        for h in range(2):
+            z_f32 = sb.tile([P, 4, HALF], F32, name="z_f32_%d" % h, tag="z_f32_%d" % h, align_bytes=64)
+            for t in range(4):
+                nc.vector.tensor_copy(z_f32[:, t, :], a_rows[t][:].indirect(n1_t[:, cols * h : cols * (h + 1)]))
+            nc.scalar.activation(
+                z_bf[:, :, 64 * h : 64 * (h + 1), :].rearrange("p r m t -> p m t r"),
+                z_f32[:].rearrange("p t (m r) -> p m t r", r=4),
+                COPY,
+            )
+        for h in range(2):
+            z2_f32 = sb.tile([P, 4, HALF], F32, name="z2_f32_%d" % h, tag="z2_f32_%d" % h, align_bytes=64)
+            for t in range(4):
+                nc.vector.tensor_tensor(
+                    z2_f32[:, t, :],
+                    b_rows[t][:].indirect(nq_t[:, cols * h : cols * (h + 1)]),
+                    b_twin[t][:, HALF * h : HALF * (h + 1)],
+                    SUB,
+                )
+            nc.scalar.activation(
+                z2_bf[:, HALF * h : HALF * (h + 1), :].rearrange("p (c i) t -> p c t i", i=4),
+                z2_f32[:].rearrange("p t (c i) -> p c t i", i=4),
+                COPY,
+                scale=-1.0,
+            )
+
+        z_w = sb.tile([P, N], U32, name="z_w", tag="z_w", align_bytes=64)
+        z_s = sb.tile([P, N], U8, name="z_s", tag="z_s", align_bytes=64)
+        z2_w = sb.tile([P, N], U32, name="z2_w", tag="z2_w", align_bytes=64)
+        z2_s = sb.tile([P, N], U8, name="z2_s", tag="z2_s", align_bytes=64)
+        nc.vector.quantize_mx(out=z_w[:].bitcast(FP8X4), scales=z_s[:], in_=z_bf[:].rearrange("p r m t -> p (r m t)"))
+        fetch_old(order[1], "b_rows3")
+        fetch_old(order[2], "b_twin3")
+        nc.vector.quantize_mx(out=z2_w[:].bitcast(FP8X4), scales=z2_s[:], in_=z2_bf[:].rearrange("p v t -> p (v t)"))
+        fetch_old(order[3], "z2_bf")
+
+        score = {}
+        for r in order:
+            score[r] = ps.tile([P, N], F32, name="score%d" % r, tag="bank%d" % r)
+            nc.tensor.matmul_mx(
+                out=score[r][:],
+                lhsT=z_w[:, P * r : P * (r + 1)].bitcast(FP8X4),
+                lhsT_scale=z_s[:, P * r : P * (r + 1)],
+                rhs=z2_w[:].bitcast(FP8X4),
+                rhs_scale=z2_s[:],
+                start=True,
+                stop=True,
+            )
+        half_s = {}
+
+        def leave_bank(r, tag):
+            half_s[r] = sb.tile([P, N], F32, name="half_s%d" % r, tag=tag, align_bytes=64)
+            nc.scalar.activation(half_s[r][:], score[r][:], COPY, scale=0.03125)
+
+        for r in order[:3]:
+            leave_bank(r, "half_s%d" % r)
+
+        y_bf = [sb.tile([P, N, 4], BF16, name="y_bf%d" % h, tag="y_bf%d" % h, align_bytes=64) for h in range(2)]
+        for r in order:
+            nc.vector.tensor_tensor(page[r][:].indirect(slot_t[:]), half_s[r][:], half_old[r][:], ADD)
+            nc.sync.dma_start(out_rows[r], page[r][:])
+            if r == order[3]:
+                nc.vector.tensor_copy(y_bf[0][:, :, r], page[r][:, 0:N])
+                nc.vector.tensor_copy(y_bf[1][:, 0:HALF, r], page[r][:, N : N + HALF])
+                nc.scalar.activation(y_bf[1][:, HALF:N, r], page[r][:, N + HALF : U], COPY)
+            else:
+                for h in range(2):
+                    nc.scalar.activation(y_bf[h][:, :, r], page[r][:, N * h : N * (h + 1)], COPY)
+            if r == order[0]:
+                leave_bank(order[3], "half_s%d" % r)
+
+        y_s = sb.tile([P, U], U8, name="y_s", tag="y_s", align_bytes=64)
+        words_out = out_1[0].rearrange("p c r -> p (c r)").bitcast(I32)
+        for h in range(2):
+            y_w = sb.tile([P, N], I32, name="y_w%d" % h, tag="y_w%d" % h, align_bytes=64)
+            nc.vector.quantize_mx(
+                out=y_w[:].bitcast(FP8X4), scales=y_s[:, N * h : N * (h + 1)], in_=y_bf[h][:].rearrange("p c r -> p (c r)")
+            )
+            nc.sync.dma_start(words_out[:, N * h : N * (h + 1)], y_w[:])
+        for q in range(4):
+            eng = nc.scalar if q % 2 else nc.sync
+            eng.dma_start(out_2[0, 4 * q : 4 * q + 4, :].bitcast(I32), y_s[32 * q : 32 * q + 4, :].bitcast(I32))

@@ -20,7 +20,7 @@ P = 128
 T = 2048
 N = 512
 U = 1024
-HALF = N // 2
+SPLIT = 640
 FLOPS = 3 * 2 * 512 * 512 * 512
 
 
@@ -33,55 +33,61 @@ def tile_picked_keyput_none_po_kernel(
         sb = ctx.enter_context(tc.tile_pool(name="sb", bufs=1))
         ps = ctx.enter_context(tc.psum_pool(name="ps", bufs=1))
 
+        def tile(name, shape, dtype, on=None):
+            return sb.tile(shape, dtype, name=name, tag=on or name, align_bytes=64)
+
         def load_list(name, src):
-            tile = lists.tile([P, N // 16], U16, name=name)
-            nc.sync.dma_start(tile[:], src)
-            return tile
+            offsets = lists.tile([P, N // 16], U16, name=name)
+            nc.sync.dma_start(offsets[:], src)
+            return offsets
 
-        def load_scale_rows(eng, tile, src):
+        def load_scale_rows(plane, src):
             for q in range(4):
-                eng.dma_start(tile[32 * q : 32 * q + 4, :].bitcast(I32), src[0, 4 * q : 4 * q + 4, :].bitcast(I32))
+                nc.sync.dma_start(plane[32 * q : 32 * q + 4, :].bitcast(I32), src[0, 4 * q : 4 * q + 4, :].bitcast(I32))
 
-        xs = sb.tile([P, T], U8, name="xs", tag="xs", align_bytes=64)
+        xs = tile("xs", [P, T], U8)
+        ws_raw = [tile("ws_raw%d" % i, [P, N], U8) for i in range(2)]
+        gains_rows = tile("gains_rows", [P, P], F32)
+        ident = tile("ident", [P, P], F32)
+        a_win = [tile("a_win%d" % t, [P, 2 * N], F32) for t in range(4)]
+        b_win = [tile("b_win%d" % t, [P, 2 * N], F32) for t in range(4)]
         nc.gpsimd.memset(xs[:].bitcast(I32), 0)
-        ws_raw = [sb.tile([P, N], U8, name="ws_raw%d" % i, tag="ws_raw%d" % i, align_bytes=64) for i in range(2)]
-        gains_rows = sb.tile([P, P], F32, name="gains_rows", tag="gains_rows", align_bytes=64)
-        nc.gpsimd.memset(gains_rows[:], 0.0)
         nc.gpsimd.memset(ws_raw[0][:].bitcast(I32), 0)
+        nc.gpsimd.memset(gains_rows[:], 0.0)
         nc.gpsimd.memset(ws_raw[1][:].bitcast(I32), 0)
-        ident = sb.tile([P, P], F32, name="ident", tag="ident", align_bytes=64)
+        nc.gpsimd.memset(b_win[0][:, N:], 0.0)
         make_identity(nc, ident[:])
+        for t in range(4):
+            nc.scalar.copy(a_win[t][:, N:], b_win[0][:, N:])
 
         offs_t = load_list("offs_t", offs)
         two_t = load_list("two_t", two)
+        load_scale_rows(xs, x_scales)
         n1_t = load_list("n1_t", n1)
+        ww_raw = [tile("ww_raw%d" % i, [P, 2 * N], U8) for i in range(2)]
+        nc.sync.dma_start(ww_raw[0][:].bitcast(I32), w1_words[0].bitcast(I32))
         nq_t = load_list("nq_t", nq)
-        slot_t = load_list("slot_t", slot)
-        ww_raw = sb.tile([P, 2 * N], U8, name="ww_raw0", tag="ww_raw", align_bytes=64)
-        nc.sync.dma_start(ww_raw[:].bitcast(I32), w1_words[0].bitcast(I32))
-        xw = sb.tile([P, T], I32, name="xw", tag="xw", align_bytes=64)
+        xw = tile("xw", [P, T], I32)
         nc.sync.dma_start(xw[:], x_words[0].rearrange("p c r -> p (c r)").bitcast(I32))
-        load_scale_rows(nc.scalar, xs, x_scales)
+        load_scale_rows(ws_raw[0], w1_scales)
         for i, g in enumerate((ga, gb)):
-            nc.scalar.dma_start(
+            nc.sync.dma_start(
                 gains_rows[4 * i : 4 * i + 4, :].rearrange("t (g q) -> t g q", q=8),
                 g.rearrange("(g t q) o -> t g (q o)", t=4, q=8),
             )
-        load_scale_rows(nc.scalar, ws_raw[0], w1_scales)
-        load_scale_rows(nc.sync, ws_raw[1], w2_scales)
-        old_rows = old.rearrange("(p t) u -> t p u", t=4)
-        out_rows = out_0.rearrange("(p t) u -> t p u", t=4)
-        order = (2, 0, 1, 3)
+        nc.sync.dma_start(ww_raw[1][:].bitcast(I32), w2_words[0].bitcast(I32))
+        load_scale_rows(ws_raw[1], w2_scales)
+        slot_t = load_list("slot_t", slot)
+        old_rows = old.rearrange("(p r) u -> r p u", r=4)
+        out_rows = out_0.rearrange("(p r) u -> r p u", r=4)
 
-        gains_ps = ps.tile([P, N], F32, name="gains_ps", tag="bank0")
+        gains_ps = ps.tile([P, N], F32, name="gains_ps", tag="bank1")
         nc.tensor.transpose(gains_ps[:, 0:P], gains_rows[:], ident[:])
-        gains = sb.tile([P, 8], F32, name="gains", tag="gains", align_bytes=64)
+        gains = tile("gains", [P, 8], F32)
         nc.scalar.copy(gains[:], gains_ps[:, 0:8])
 
-        picked_w = [sb.tile([P, N], U32, name="picked_w0", tag="picked_w0", align_bytes=64)]
-        picked_s = [sb.tile([P, N], U8, name="picked_s%d" % i, tag="picked_s%d" % i, align_bytes=64) for i in range(2)]
-        ww = [sb.tile([P, 2 * N], U8, name="ww%d" % i, tag="ww%d" % i, align_bytes=64) for i in range(2)]
-        ws = [sb.tile([P, N], U8, name="ws%d" % i, tag="ws%d" % i, align_bytes=64) for i in range(2)]
+        picked_s = [tile("picked_s%d" % i, [P, N], U8) for i in range(2)]
+        ww = [tile("ww%d" % i, [P, 2 * N], U8) for i in range(2)]
 
         def deal(dst, src, run):
             nc.vector.tensor_copy(
@@ -89,101 +95,77 @@ def tile_picked_keyput_none_po_kernel(
                 src[:].bitcast(I32).rearrange("p (g t q) -> p t g q", t=4, q=run),
             )
 
-        def project(i, bank0):
+        for i, lst in enumerate((offs_t, two_t)):
+            nc.vector.tensor_copy(picked_s[i][:], xs[:].indirect(lst[:]))
+        proj = []
+        for i, (lst, on, on_s) in enumerate(((offs_t, None, None), (two_t, "ws_raw0", "xw"))):
+            picked_w = tile("picked_w%d" % i, [P, N], U32, on)
+            deal(ww[i], ww_raw[i], 4)
+            nc.vector.tensor_copy(picked_w[:], xw[:].bitcast(U32).indirect(lst[:]))
+            ws = tile("ws%d" % i, [P, N], U8, on_s)
+            deal(ws, ws_raw[i], 2)
             banks = []
             for t in range(4):
-                bank = ps.tile([P, N], F32, name="proj%d_%d" % (i, t), tag="bank%d" % (bank0 + t))
+                bank = ps.tile([P, N], F32, name="proj%d_%d" % (i, t), tag="bank%d" % (4 * i + t))
                 nc.tensor.matmul_mx(
                     out=bank[:],
                     lhsT=ww[i][:, 2 * P * t : 2 * P * (t + 1)].bitcast(FP4X4),
-                    lhsT_scale=ws[i][:, P * t : P * (t + 1)],
-                    rhs=picked_w[i][:].bitcast(FP8X4),
+                    lhsT_scale=ws[:, P * t : P * (t + 1)],
+                    rhs=picked_w[:].bitcast(FP8X4),
                     rhs_scale=picked_s[i][:],
                     start=True,
                     stop=True,
                 )
                 banks.append(bank)
-            return banks
+            proj.append(banks)
 
-        for i, lst in enumerate((offs_t, two_t)):
-            nc.vector.tensor_copy(picked_s[i][:], xs[:].indirect(lst[:]))
-        nc.vector.tensor_copy(picked_w[0][:], xw[:].bitcast(U32).indirect(offs_t[:]))
-        deal(ww[0], ww_raw, 4)
-        ww_raw = sb.tile([P, 2 * N], U8, name="ww_raw1", tag="ww_raw", align_bytes=64)
-        nc.sync.dma_start(ww_raw[:].bitcast(I32), w2_words[0].bitcast(I32))
-        deal(ws[0], ws_raw[0], 2)
-        a_banks = project(0, 0)
-        picked_w.append(sb.tile([P, N], U32, name="picked_w1", tag="ws_raw0", align_bytes=64))
-        nc.vector.tensor_copy(picked_w[1][:], xw[:].bitcast(U32).indirect(two_t[:]))
-        deal(ww[1], ww_raw, 4)
-        deal(ws[1], ws_raw[1], 2)
-        b_banks = project(1, 4)
-
-        page = {}
-        for r, tag in zip(order, ("xs", "gains_rows", "xw", "ww_raw")):
-            page[r] = sb.tile([P, U], F32, name="page%d" % r, tag=tag, align_bytes=64)
+        page = []
+        for r in range(4):
+            page.append(tile("page%d" % r, [P, U], F32))
             nc.sync.dma_start(page[r][:], old_rows[r])
 
-        a_rows = [sb.tile([P, N], F32, name="a_rows%d" % t, tag="a_rows%d" % t, align_bytes=64) for t in range(4)]
-        b_rows = [sb.tile([P, N], F32, name="b_rows%d" % t, tag="b_rows%d" % t, align_bytes=64) for t in range(4)]
-        b_twin = [sb.tile([P, N], F32, name="b_twin%d" % t, tag="b_twin%d" % t, align_bytes=64) for t in range(4)]
+        last_twin = tile("last_twin", [P, N], F32)
+        b_twin = [b_win[t + 1][:, N:] for t in range(3)] + [last_twin[:]]
         for t in range(4):
-            nc.scalar.activation(a_rows[t][:], a_banks[t][:], COPY, scale=gains[:, t : t + 1])
+            nc.scalar.activation(a_win[t][:, :N], proj[0][t][:], COPY, scale=gains[:, t : t + 1])
         for t in range(4):
-            nc.scalar.activation(b_rows[t][:], b_banks[t][:], COPY, scale=gains[:, 4 + t : 5 + t])
-            nc.scalar.activation(b_twin[t][:], b_banks[t][:], COPY, scale=gains[:, 4 + t : 5 + t])
+            nc.scalar.activation(b_win[t][:, :N], proj[1][t][:], COPY, scale=gains[:, 4 + t : 5 + t])
+            nc.scalar.activation(b_twin[t], proj[1][t][:], COPY, scale=gains[:, 4 + t : 5 + t])
 
-        half_old = {}
+        z_f32 = tile("z_f32", [P, 4, N], F32, "ws_raw1")
+        z2_f32 = tile("z2_f32", [P, 4, N], F32)
+        z_bf = tile("z_bf", [P, 4, P, 4], BF16)
+        z2_bf = tile("z2_bf", [P, N, 4], BF16)
+        for t in range(4):
+            nc.vector.tensor_copy(z_f32[:, t, :], a_win[t][:].indirect(n1_t[:]))
+        nc.scalar.activation(z_bf[:].rearrange("p r m t -> p m t r"), z_f32[:].rearrange("p t (m r) -> p m t r", r=4), COPY)
+        for t in range(4):
+            nc.vector.tensor_tensor(z2_f32[:, t, :], b_win[t][:].indirect(nq_t[:]), b_twin[t], SUB)
+        nc.scalar.activation(
+            z2_bf[:].rearrange("p (c i) t -> p c t i", i=4), z2_f32[:].rearrange("p t (c i) -> p c t i", i=4), COPY, scale=-1.0
+        )
 
-        def fetch_old(t, tag):
-            half_old[t] = sb.tile([P, N], F32, name="half_old%d" % t, tag=tag, align_bytes=64)
-            nc.vector.tensor_scalar(half_old[t][:], page[t][:].indirect(slot_t[:]), 0.5, 0.0, MULT, ADD)
+        half_old = []
 
-        fetch_old(order[0], "half_old")
+        def fetch_old(r, on):
+            half_old.append(tile("half_old%d" % r, [P, N], F32, on))
+            nc.vector.tensor_scalar(half_old[r][:], page[r][:].indirect(slot_t[:]), 0.5, 0.0, MULT, ADD)
 
-        z_bf = sb.tile([P, 4, P, 4], BF16, name="z_bf", tag="z_bf", align_bytes=64)
-        z2_bf = sb.tile([P, N, 4], BF16, name="z2_bf", tag="z2_bf", align_bytes=64)
-        cols = HALF // 16
-        for h in range(2):
-            z_f32 = sb.tile([P, 4, HALF], F32, name="z_f32_%d" % h, tag="z_f32_%d" % h, align_bytes=64)
-            for t in range(4):
-                nc.vector.tensor_copy(z_f32[:, t, :], a_rows[t][:].indirect(n1_t[:, cols * h : cols * (h + 1)]))
-            nc.scalar.activation(
-                z_bf[:, :, 64 * h : 64 * (h + 1), :].rearrange("p r m t -> p m t r"),
-                z_f32[:].rearrange("p t (m r) -> p m t r", r=4),
-                COPY,
-            )
-        for h in range(2):
-            z2_f32 = sb.tile([P, 4, HALF], F32, name="z2_f32_%d" % h, tag="z2_f32_%d" % h, align_bytes=64)
-            for t in range(4):
-                nc.vector.tensor_tensor(
-                    z2_f32[:, t, :],
-                    b_rows[t][:].indirect(nq_t[:, cols * h : cols * (h + 1)]),
-                    b_twin[t][:, HALF * h : HALF * (h + 1)],
-                    SUB,
-                )
-            nc.scalar.activation(
-                z2_bf[:, HALF * h : HALF * (h + 1), :].rearrange("p (c i) t -> p c t i", i=4),
-                z2_f32[:].rearrange("p t (c i) -> p c t i", i=4),
-                COPY,
-                scale=-1.0,
-            )
-
-        z_w = sb.tile([P, N], U32, name="z_w", tag="z_w", align_bytes=64)
-        z_s = sb.tile([P, N], U8, name="z_s", tag="z_s", align_bytes=64)
-        z2_w = sb.tile([P, N], U32, name="z2_w", tag="z2_w", align_bytes=64)
-        z2_s = sb.tile([P, N], U8, name="z2_s", tag="z2_s", align_bytes=64)
+        z_w = tile("z_w", [P, N], U32)
+        z_s = tile("z_s", [P, N], U8)
+        z2_w = tile("z2_w", [P, N], U32)
+        z2_s = tile("z2_s", [P, N], U8)
         nc.vector.quantize_mx(out=z_w[:].bitcast(FP8X4), scales=z_s[:], in_=z_bf[:].rearrange("p r m t -> p (r m t)"))
-        fetch_old(order[1], "b_rows3")
-        fetch_old(order[2], "b_twin3")
+        for r, on in enumerate(("ws_raw1", "b_win3", "last_twin")):
+            fetch_old(r, on)
         nc.vector.quantize_mx(out=z2_w[:].bitcast(FP8X4), scales=z2_s[:], in_=z2_bf[:].rearrange("p v t -> p (v t)"))
-        fetch_old(order[3], "z2_bf")
+        fetch_old(3, "z2_bf")
 
-        score = {}
-        for r in order:
-            score[r] = ps.tile([P, N], F32, name="score%d" % r, tag="bank%d" % r)
+        half_s = [tile("half_s%d" % r, [P, N], F32) for r in range(4)]
+        for r in range(4):
+            score = ps.tile([P, N], F32, name="score%d" % r, tag="bank%d" % r)
             nc.tensor.matmul_mx(
-                out=score[r][:],
+                out=score[:],
                 lhsT=z_w[:, P * r : P * (r + 1)].bitcast(FP8X4),
                 lhsT_scale=z_s[:, P * r : P * (r + 1)],
                 rhs=z2_w[:].bitcast(FP8X4),
@@ -191,37 +173,30 @@ def tile_picked_keyput_none_po_kernel(
                 start=True,
                 stop=True,
             )
-        half_s = {}
+            nc.scalar.activation(half_s[r][:], score[:], COPY, scale=0.03125)
 
-        def leave_bank(r, tag):
-            half_s[r] = sb.tile([P, N], F32, name="half_s%d" % r, tag=tag, align_bytes=64)
-            nc.scalar.activation(half_s[r][:], score[r][:], COPY, scale=0.03125)
-
-        for r in order[:3]:
-            leave_bank(r, "half_s%d" % r)
-
-        y_bf = [sb.tile([P, N, 4], BF16, name="y_bf%d" % h, tag="y_bf%d" % h, align_bytes=64) for h in range(2)]
-        for r in order:
+        y_bf = tile("y_bf", [P, U, 4], BF16)
+        for r in range(4):
             nc.vector.tensor_tensor(page[r][:].indirect(slot_t[:]), half_s[r][:], half_old[r][:], ADD)
             nc.sync.dma_start(out_rows[r], page[r][:])
-            if r == order[3]:
-                nc.vector.tensor_copy(y_bf[0][:, :, r], page[r][:, 0:N])
-                nc.vector.tensor_copy(y_bf[1][:, 0:HALF, r], page[r][:, N : N + HALF])
-                nc.scalar.activation(y_bf[1][:, HALF:N, r], page[r][:, N + HALF : U], COPY)
-            else:
-                for h in range(2):
-                    nc.scalar.activation(y_bf[h][:, :, r], page[r][:, N * h : N * (h + 1)], COPY)
-            if r == order[0]:
-                leave_bank(order[3], "half_s%d" % r)
+            if r < 2:
+                nc.scalar.activation(y_bf[:, :, r], page[r][:], COPY)
+            elif r == 2:
+                nc.scalar.activation(y_bf[:, :SPLIT, 2:4], page[r][:, :SPLIT].unsqueeze(2).to_broadcast([P, SPLIT, 2]), COPY)
+                nc.scalar.activation(y_bf[:, SPLIT:, r], page[r][:, SPLIT:], COPY)
+        nc.scalar.activation(y_bf[:, SPLIT:, 3], page[3][:, SPLIT:], COPY)
+        for cols in (slice(0, N), slice(N, SPLIT)):
+            nc.vector.tensor_copy(y_bf[:, cols, 3], page[3][:, cols])
 
-        y_s = sb.tile([P, U], U8, name="y_s", tag="y_s", align_bytes=64)
+        y_s = tile("y_s", [P, U], U8)
         words_out = out_1[0].rearrange("p c r -> p (c r)").bitcast(I32)
         for h in range(2):
-            y_w = sb.tile([P, N], I32, name="y_w%d" % h, tag="y_w%d" % h, align_bytes=64)
+            cols = slice(N * h, N * (h + 1))
+            y_w = tile("y_w%d" % h, [P, N], I32)
             nc.vector.quantize_mx(
-                out=y_w[:].bitcast(FP8X4), scales=y_s[:, N * h : N * (h + 1)], in_=y_bf[h][:].rearrange("p c r -> p (c r)")
+                out=y_w[:].bitcast(FP8X4), scales=y_s[:, cols], in_=y_bf[:, cols, :].rearrange("p c r -> p (c r)")
             )
-            nc.sync.dma_start(words_out[:, N * h : N * (h + 1)], y_w[:])
+            nc.sync.dma_start(words_out[:, cols], y_w[:])
         for q in range(4):
             eng = nc.scalar if q % 2 else nc.sync
             eng.dma_start(out_2[0, 4 * q : 4 * q + 4, :].bitcast(I32), y_s[32 * q : 32 * q + 4, :].bitcast(I32))

@@ -52,8 +52,8 @@ def tile_picked_keyput_none_po_kernel(
         a_win = [tile("a_win%d" % t, [P, 2 * N], F32) for t in range(4)]
         b_win = [tile("b_win%d" % t, [P, 2 * N], F32) for t in range(4)]
         nc.gpsimd.memset(xs[:].bitcast(I32), 0)
-        nc.gpsimd.memset(ws_raw[0][:].bitcast(I32), 0)
         nc.gpsimd.memset(gains_rows[:], 0.0)
+        nc.gpsimd.memset(ws_raw[0][:].bitcast(I32), 0)
         nc.gpsimd.memset(ws_raw[1][:].bitcast(I32), 0)
         nc.gpsimd.memset(b_win[0][:, N:], 0.0)
         make_identity(nc, ident[:])
@@ -66,27 +66,26 @@ def tile_picked_keyput_none_po_kernel(
         n1_t = load_list("n1_t", n1)
         ww_raw = [tile("ww_raw%d" % i, [P, 2 * N], U8) for i in range(2)]
         nc.sync.dma_start(ww_raw[0][:].bitcast(I32), w1_words[0].bitcast(I32))
-        nq_t = load_list("nq_t", nq)
         xw = tile("xw", [P, T], I32)
         nc.sync.dma_start(xw[:], x_words[0].rearrange("p c r -> p (c r)").bitcast(I32))
-        load_scale_rows(ws_raw[0], w1_scales)
         for i, g in enumerate((ga, gb)):
             nc.sync.dma_start(
                 gains_rows[4 * i : 4 * i + 4, :].rearrange("t (g q) -> t g q", q=8),
                 g.rearrange("(g t q) o -> t g (q o)", t=4, q=8),
             )
+        load_scale_rows(ws_raw[0], w1_scales)
         nc.sync.dma_start(ww_raw[1][:].bitcast(I32), w2_words[0].bitcast(I32))
         load_scale_rows(ws_raw[1], w2_scales)
+        nq_t = load_list("nq_t", nq)
         slot_t = load_list("slot_t", slot)
         old_rows = old.rearrange("(p r) u -> r p u", r=4)
         out_rows = out_0.rearrange("(p r) u -> r p u", r=4)
 
-        gains_ps = ps.tile([P, N], F32, name="gains_ps", tag="bank1")
+        gains_ps = ps.tile([P, N], F32, name="gains_ps", tag="bank7")
         nc.tensor.transpose(gains_ps[:, 0:P], gains_rows[:], ident[:])
         gains = tile("gains", [P, 8], F32)
         nc.scalar.copy(gains[:], gains_ps[:, 0:8])
 
-        picked_s = [tile("picked_s%d" % i, [P, N], U8) for i in range(2)]
         ww = [tile("ww%d" % i, [P, 2 * N], U8) for i in range(2)]
 
         def deal(dst, src, run):
@@ -95,14 +94,15 @@ def tile_picked_keyput_none_po_kernel(
                 src[:].bitcast(I32).rearrange("p (g t q) -> p t g q", t=4, q=run),
             )
 
+        picked_s = [tile("picked_s%d" % i, [P, N], U8) for i in range(2)]
         for i, lst in enumerate((offs_t, two_t)):
             nc.vector.tensor_copy(picked_s[i][:], xs[:].indirect(lst[:]))
         proj = []
-        for i, (lst, on, on_s) in enumerate(((offs_t, None, None), (two_t, "ws_raw0", "xw"))):
+        for i, (lst, on, on_s) in enumerate(((offs_t, None, "gains_rows"), (two_t, "ws_raw0", "xw"))):
             picked_w = tile("picked_w%d" % i, [P, N], U32, on)
-            deal(ww[i], ww_raw[i], 4)
             nc.vector.tensor_copy(picked_w[:], xw[:].bitcast(U32).indirect(lst[:]))
             ws = tile("ws%d" % i, [P, N], U8, on_s)
+            deal(ww[i], ww_raw[i], 4)
             deal(ws, ws_raw[i], 2)
             banks = []
             for t in range(4):
@@ -156,9 +156,10 @@ def tile_picked_keyput_none_po_kernel(
         z2_w = tile("z2_w", [P, N], U32)
         z2_s = tile("z2_s", [P, N], U8)
         nc.vector.quantize_mx(out=z_w[:].bitcast(FP8X4), scales=z_s[:], in_=z_bf[:].rearrange("p r m t -> p (r m t)"))
-        for r, on in enumerate(("ws_raw1", "b_win3", "last_twin")):
+        for r, on in enumerate(("b_win3", "last_twin")):
             fetch_old(r, on)
         nc.vector.quantize_mx(out=z2_w[:].bitcast(FP8X4), scales=z2_s[:], in_=z2_bf[:].rearrange("p v t -> p (v t)"))
+        fetch_old(2, "z2_f32")
         fetch_old(3, "z2_bf")
 
         half_s = [tile("half_s%d" % r, [P, N], F32) for r in range(4)]
@@ -190,9 +191,9 @@ def tile_picked_keyput_none_po_kernel(
 
         y_s = tile("y_s", [P, U], U8)
         words_out = out_1[0].rearrange("p c r -> p (c r)").bitcast(I32)
-        for h in range(2):
-            cols = slice(N * h, N * (h + 1))
-            y_w = tile("y_w%d" % h, [P, N], I32)
+        for c0, c1 in ((0, 512), (512, 768), (768, 1024)):
+            cols = slice(c0, c1)
+            y_w = tile("y_w%d" % c0, [P, c1 - c0], I32)
             nc.vector.quantize_mx(
                 out=y_w[:].bitcast(FP8X4), scales=y_s[:, cols], in_=y_bf[:, cols, :].rearrange("p c r -> p (c r)")
             )

from contextlib import ExitStack

import concourse.mybir as mybir
from concourse.masks import make_identity

F32 = mybir.dt.float32
BF16 = mybir.dt.bfloat16
I32 = mybir.dt.int32
U32 = mybir.dt.uint32
U16 = mybir.dt.uint16
U8 = mybir.dt.uint8
FP8X4 = mybir.dt.float8_e4m3fn_x4
FP4X4 = mybir.dt.float4_e2m1fn_x4
COPY = mybir.ActivationFunctionType.Copy
MULT = mybir.AluOpType.mult
ADD = mybir.AluOpType.add
SUB = mybir.AluOpType.subtract

P = 128
T = 2048
N = 512
U = 1024
SPLIT = 640
FLOPS = 3 * 2 * 512 * 512 * 512


def tile_picked_keyput_none_po_kernel(
    tc, x_words, x_scales, w1_words, w1_scales, w2_words, w2_scales, ga, gb, old, offs, two, n1, nq, slot, out_0, out_1, out_2
):
    nc = tc.nc
    with ExitStack() as ctx:
        lists = ctx.enter_context(tc.tile_pool(name="lists", bufs=1))
        sb = ctx.enter_context(tc.tile_pool(name="sb", bufs=1))
        ps = ctx.enter_context(tc.psum_pool(name="ps", bufs=1))

        def tile(name, shape, dtype, on=None):
            return sb.tile(shape, dtype, name=name, tag=on or name, align_bytes=64)

        def load_list(name, src):
            offsets = lists.tile([P, N // 16], U16, name=name)
            nc.sync.dma_start(offsets[:], src)
            return offsets

        def load_scale_rows(plane, src):
            for q in range(4):
                nc.sync.dma_start(plane[32 * q : 32 * q + 4, :].bitcast(I32), src[0, 4 * q : 4 * q + 4, :].bitcast(I32))

        xs = tile("xs", [P, T], U8)
        ws_raw = [tile("ws_raw%d" % i, [P, N], U8) for i in range(2)]
        gains_rows = tile("gains_rows", [P, P], F32)
        ident = tile("ident", [P, P], F32)
        a_win = [tile("a_win%d" % t, [P, 2 * N], F32) for t in range(4)]
        b_win = [tile("b_win%d" % t, [P, 2 * N], F32) for t in range(4)]
        nc.gpsimd.memset(xs[:].bitcast(I32), 0)
        nc.gpsimd.memset(gains_rows[:], 0.0)
        nc.gpsimd.memset(ws_raw[0][:].bitcast(I32), 0)
        nc.gpsimd.memset(ws_raw[1][:].bitcast(I32), 0)
        nc.gpsimd.memset(b_win[0][:, N:], 0.0)
        make_identity(nc, ident[:])
        for t in range(4):
            nc.scalar.copy(a_win[t][:, N:], b_win[0][:, N:])

        offs_t = load_list("offs_t", offs)
        two_t = load_list("two_t", two)
        load_scale_rows(xs, x_scales)
        n1_t = load_list("n1_t", n1)
        ww_raw = [tile("ww_raw%d" % i, [P, 2 * N], U8) for i in range(2)]
        nc.sync.dma_start(ww_raw[0][:].bitcast(I32), w1_words[0].bitcast(I32))
        xw = tile("xw", [P, T], I32)
        nc.sync.dma_start(xw[:], x_words[0].rearrange("p c r -> p (c r)").bitcast(I32))
        for i, g in enumerate((ga, gb)):
            nc.sync.dma_start(
                gains_rows[4 * i : 4 * i + 4, :].rearrange("t (g q) -> t g q", q=8),
                g.rearrange("(g t q) o -> t g (q o)", t=4, q=8),
            )
        load_scale_rows(ws_raw[0], w1_scales)
        nc.sync.dma_start(ww_raw[1][:].bitcast(I32), w2_words[0].bitcast(I32))
        load_scale_rows(ws_raw[1], w2_scales)
        nq_t = load_list("nq_t", nq)
        slot_t = load_list("slot_t", slot)
        old_rows = old.rearrange("(p r) u -> r p u", r=4)
        out_rows = out_0.rearrange("(p r) u -> r p u", r=4)

        gains_ps = ps.tile([P, N], F32, name="gains_ps", tag="bank7")
        nc.tensor.transpose(gains_ps[:, 0:P], gains_rows[:], ident[:])
        gains = tile("gains", [P, 8], F32)
        nc.scalar.copy(gains[:], gains_ps[:, 0:8])

        ww = [tile("ww%d" % i, [P, 2 * N], U8) for i in range(2)]

        def deal(dst, src, run):
            nc.vector.tensor_copy(
                dst[:].bitcast(I32).rearrange("p (t g q) -> p t g q", t=4, q=run),
                src[:].bitcast(I32).rearrange("p (g t q) -> p t g q", t=4, q=run),
            )

        picked_s = [tile("picked_s%d" % i, [P, N], U8) for i in range(2)]
        for i, lst in enumerate((offs_t, two_t)):
            nc.vector.tensor_copy(picked_s[i][:], xs[:].indirect(lst[:]))
        proj = []
        for i, (lst, on, on_s) in enumerate(((offs_t, None, "gains_rows"), (two_t, "ws_raw0", "xw"))):
            picked_w = tile("picked_w%d" % i, [P, N], U32, on)
            nc.vector.tensor_copy(picked_w[:], xw[:].bitcast(U32).indirect(lst[:]))
            ws = tile("ws%d" % i, [P, N], U8, on_s)
            deal(ww[i], ww_raw[i], 4)
            deal(ws, ws_raw[i], 2)
            banks = []
            for t in range(4):
                bank = ps.tile([P, N], F32, name="proj%d_%d" % (i, t), tag="bank%d" % (4 * i + t))
                nc.tensor.matmul_mx(
                    out=bank[:],
                    lhsT=ww[i][:, 2 * P * t : 2 * P * (t + 1)].bitcast(FP4X4),
                    lhsT_scale=ws[:, P * t : P * (t + 1)],
                    rhs=picked_w[:].bitcast(FP8X4),
                    rhs_scale=picked_s[i][:],
                    start=True,
                    stop=True,
                )
                banks.append(bank)
            proj.append(banks)

        page = []
        for r in range(4):
            page.append(tile("page%d" % r, [P, U], F32))
            nc.sync.dma_start(page[r][:], old_rows[r])

        last_twin = tile("last_twin", [P, N], F32)
        b_twin = [b_win[t + 1][:, N:] for t in range(3)] + [last_twin[:]]
        for t in range(4):
            nc.scalar.activation(a_win[t][:, :N], proj[0][t][:], COPY, scale=gains[:, t : t + 1])
        for t in range(4):
            nc.scalar.activation(b_win[t][:, :N], proj[1][t][:], COPY, scale=gains[:, 4 + t : 5 + t])
            nc.scalar.activation(b_twin[t], proj[1][t][:], COPY, scale=gains[:, 4 + t : 5 + t])

        z_f32 = tile("z_f32", [P, 4, N], F32, "ws_raw1")
        z2_f32 = tile("z2_f32", [P, 4, N], F32)
        z_bf = tile("z_bf", [P, 4, P, 4], BF16)
        z2_bf = tile("z2_bf", [P, N, 4], BF16)
        for t in range(4):
            nc.vector.tensor_copy(z_f32[:, t, :], a_win[t][:].indirect(n1_t[:]))
        nc.scalar.activation(z_bf[:].rearrange("p r m t -> p m t r"), z_f32[:].rearrange("p t (m r) -> p m t r", r=4), COPY)
        for t in range(4):
            nc.vector.tensor_tensor(z2_f32[:, t, :], b_win[t][:].indirect(nq_t[:]), b_twin[t], SUB)
        nc.scalar.activation(
            z2_bf[:].rearrange("p (c i) t -> p c t i", i=4), z2_f32[:].rearrange("p t (c i) -> p c t i", i=4), COPY, scale=-1.0
        )

        half_old = []

        def fetch_old(r, on):
            half_old.append(tile("half_old%d" % r, [P, N], F32, on))
            nc.vector.tensor_scalar(half_old[r][:], page[r][:].indirect(slot_t[:]), 0.5, 0.0, MULT, ADD)

        z_w = tile("z_w", [P, N], U32)
        z_s = tile("z_s", [P, N], U8)
        z2_w = tile("z2_w", [P, N], U32)
        z2_s = tile("z2_s", [P, N], U8)
        nc.vector.quantize_mx(out=z_w[:].bitcast(FP8X4), scales=z_s[:], in_=z_bf[:].rearrange("p r m t -> p (r m t)"))
        for r, on in enumerate(("b_win3", "last_twin")):
            fetch_old(r, on)
        nc.vector.quantize_mx(out=z2_w[:].bitcast(FP8X4), scales=z2_s[:], in_=z2_bf[:].rearrange("p v t -> p (v t)"))
        fetch_old(2, "z2_f32")
        fetch_old(3, "z2_bf")

        half_s = [tile("half_s%d" % r, [P, N], F32) for r in range(4)]
        for r in range(4):
            score = ps.tile([P, N], F32, name="score%d" % r, tag="bank%d" % r)
            nc.tensor.matmul_mx(
                out=score[:],
                lhsT=z_w[:, P * r : P * (r + 1)].bitcast(FP8X4),
                lhsT_scale=z_s[:, P * r : P * (r + 1)],
                rhs=z2_w[:].bitcast(FP8X4),
                rhs_scale=z2_s[:],
                start=True,
                stop=True,
            )
            nc.scalar.activation(half_s[r][:], score[:], COPY, scale=0.03125)

        y_bf = tile("y_bf", [P, U, 4], BF16)
        for r in range(4):
            nc.vector.tensor_tensor(page[r][:].indirect(slot_t[:]), half_s[r][:], half_old[r][:], ADD)
            nc.sync.dma_start(out_rows[r], page[r][:])
            if r < 2:
                nc.scalar.activation(y_bf[:, :, r], page[r][:], COPY)
            elif r == 2:
                nc.scalar.activation(y_bf[:, :SPLIT, 2:4], page[r][:, :SPLIT].unsqueeze(2).to_broadcast([P, SPLIT, 2]), COPY)
                nc.scalar.activation(y_bf[:, SPLIT:, r], page[r][:, SPLIT:], COPY)
        nc.scalar.activation(y_bf[:, SPLIT:, 3], page[3][:, SPLIT:], COPY)
        for cols in (slice(0, N), slice(N, SPLIT)):
            nc.vector.tensor_copy(y_bf[:, cols, 3], page[3][:, cols])

        y_s = tile("y_s", [P, U], U8)
        words_out = out_1[0].rearrange("p c r -> p (c r)").bitcast(I32)
        for c0, c1 in ((0, 512), (512, 768), (768, 1024)):
            cols = slice(c0, c1)
            y_w = tile("y_w%d" % c0, [P, c1 - c0], I32)
            nc.vector.quantize_mx(
                out=y_w[:].bitcast(FP8X4), scales=y_s[:, cols], in_=y_bf[:, cols, :].rearrange("p c r -> p (c r)")
            )
            nc.sync.dma_start(words_out[:, cols], y_w[:])
        for q in range(4):
            eng = nc.scalar if q % 2 else nc.sync
            eng.dma_start(out_2[0, 4 * q : 4 * q + 4, :].bitcast(I32), y_s[32 * q : 32 * q + 4, :].bitcast(I32))
